import numpy as np
import ml_dtypes


def mxq(x, axis, fmt="e4m3"):
    dtype, down = {"e4m3": (ml_dtypes.float8_e4m3fn, 7), "e5m2": (ml_dtypes.float8_e5m2, 14)}[fmt]
    v = np.moveaxis(np.asarray(x, np.float32).astype(ml_dtypes.bfloat16).astype(np.float64), axis, -1)
    blocks = v.reshape(v.shape[:-1] + (-1, 32))
    amax = np.abs(blocks).max(-1, keepdims=True)
    byte = np.maximum(np.where(amax > 0, np.frexp(amax)[1] - 1 + 127, 0) - down, 1)
    scale = np.exp2(byte - 127.0)
    codes = (blocks / scale).astype(np.float32).astype(dtype).astype(np.float64)
    return np.moveaxis((codes * scale).reshape(v.shape), -1, axis)


WIDE = False


def mx_kscale(k):
    if not WIDE:
        return np.ones(k)
    levels = np.array([10, -10, 5, -5, 0])
    if k % 512:
        return np.exp2(np.random.permutation(np.resize(levels, k // 32))).repeat(32)
    a = np.empty((k // 512, 16))
    for p in range(k // 512):
        a[p, :8] = np.random.permutation(np.resize(levels, 8))
        for g in range(8):
            far = levels[np.abs(levels - a[p, g]) >= 10]
            a[p, g + 8] = far[np.random.randint(len(far))]
    return np.exp2(a.ravel()).repeat(32)


def f64(x):
    return np.asarray(x).astype(np.float64)


def striped(idx):
    return np.tile(np.asarray(idx).reshape(-1, 16).T, (8, 1)).astype(np.uint16)


def unstriped(offs):
    return offs[:16].T.reshape(-1).astype(np.int64)


E2M1 = np.array([0.0, 0.5, 1.0, 1.5, 2.0, 3.0, 4.0, 6.0, -0.0, -0.5, -1.0, -1.5, -2.0, -3.0, -4.0, -6.0])


def pack_weight(w, fmt):
    k, n = w.shape
    w = f64(np.asarray(w, np.float32).astype(ml_dtypes.bfloat16)).reshape(k // 32, 32, n)
    amax = np.abs(w).max(1)
    if fmt == "e4m3":
        byte = np.frexp(amax)[1] - 1 + 127 - 7
    else:
        mant, ex = np.frexp(amax / 6.0)
        byte = np.where(mant > 0.5, ex, ex - 1) + 127
    byte = np.clip(np.where(amax > 0, byte, 1), 1, 254)
    scaled = (w * np.exp2(127.0 - byte)[:, None, :]).reshape(k, n).astype(np.float32)
    by_word = np.ascontiguousarray(scaled.reshape(k // 512, 128, 4, n).transpose(0, 1, 3, 2))
    if fmt == "e4m3":
        words = by_word.astype(ml_dtypes.float8_e4m3fn).view(np.uint8)
    else:
        c = by_word.astype(ml_dtypes.float4_e2m1fn).view(np.uint8) & 0xF
        words = (c[..., 0::2] | (c[..., 1::2] << 4)).reshape(k // 512, 128, 2 * n)
    return np.ascontiguousarray(words), np.ascontiguousarray(byte.astype(np.uint8).reshape(k // 512, 16, n))


def unpack_weight(words, scales, fmt):
    g, _, n = scales.shape
    words = np.ascontiguousarray(words).reshape(g, 128, n, -1)
    if fmt == "e4m3":
        vals = words.view(ml_dtypes.float8_e4m3fn).astype(np.float64)
    else:
        nib = np.empty((g, 128, n, 4), np.uint8)
        nib[..., 0::2] = words & 0xF
        nib[..., 1::2] = words >> 4
        vals = E2M1[nib]
    vals = vals * np.repeat(np.exp2(scales.astype(np.float64) - 127.0), 8, axis=1)[..., None]
    return vals.transpose(0, 1, 3, 2).reshape(g * 512, n)


def sigmoid(v):
    return 1.0 / (1.0 + np.exp(-v))


D, T, I, Q, E, U, V = 512, 2048, 512, 128, 512, 512, 256


def setup_inputs():
    n = np.random.standard_normal
    idx = np.random.permutation(T)[:I]
    idx2 = np.random.randint(0, U, I)
    idx3 = np.random.randint(0, V, I)
    fd = mx_kscale(D)
    fi = mx_kscale(I)
    ti = np.ones(T)
    ti[idx] = fi
    keysp = pack_weight(n((D, T)) / fd[:, None], "e4m3")
    return {
        "query": (n((D, Q)) * 0.25 / np.sqrt(D) * fd[:, None]).astype(np.float32),
        "keys_words": keysp[0],
        "keys_scales": keysp[1],
        "pquery": (n((D, Q)) * 1.0 / np.sqrt(D) * fd[:, None]).astype(np.float32),
        "pgsum": (n((D, U)) / fd[:, None]).astype(np.float32),
        "vquery": (n((D, Q)) * 1.0 / np.sqrt(D) * fd[:, None]).astype(np.float32),
        "vlsum": (n((D, V)) / fd[:, None]).astype(np.float32),
        "size": (np.random.uniform(0.5, 2.0, (1, I)) * fi).astype(np.float32),
        "vals": (n((E, T)) / ti).astype(np.float32),
        "offs": striped(idx),
        "offs2": striped(idx2),
        "offs3": striped(idx3),
    }


def reference(query, keys_words, keys_scales, pquery, pgsum, vquery, vlsum, size, vals, offs, offs2, offs3):
    idx = unstriped(offs)
    idx2 = unstriped(offs2)
    idx3 = unstriped(offs3)
    keysu = unpack_weight(keys_words, keys_scales, "e4m3")
    queryq = mxq(f64(query), 0, "e4m3")
    keysidxg = keysu[:, idx]
    a = queryq.T @ keysidxg
    pqueryq = mxq(f64(pquery), 0, "e4m3")
    pgsumq = mxq(f64(pgsum), 0, "e4m3")
    b = pqueryq.T @ pgsumq
    vqueryq = mxq(f64(vquery), 0, "e4m3")
    vlsumq = mxq(f64(vlsum), 0, "e4m3")
    g = vqueryq.T @ vlsumq
    p = np.exp(a - np.max(a, axis=1, keepdims=True)) * sigmoid(b[:, idx2]) * sigmoid(g[:, idx3])
    w = p * f64(size) / np.sum(p, axis=1, keepdims=True)
    wt = w.T
    vt = f64(vals)[:, idx].T
    wtq = mxq(wt, 0, "e4m3")
    vtq = mxq(vt, 0, "e4m3")
    o = wtq.T @ vtq
    return o

@@ -1,0 +1,221 @@
+from contextlib import ExitStack
+
+import concourse.mybir as mybir
+from concourse.masks import make_identity
+
+D, T, I, Q, E, U, V = 512, 2048, 512, 128, 512, 512, 256
+FLOPS = 2 * Q * (D * I + D * U + D * V + I * E)
+
+F32 = mybir.dt.float32
+BF16 = mybir.dt.bfloat16
+I32 = mybir.dt.int32
+U32 = mybir.dt.uint32
+U16 = mybir.dt.uint16
+U8 = mybir.dt.uint8
+FP8X4 = mybir.dt.float8_e4m3fn_x4
+ACT = mybir.ActivationFunctionType
+ALU = mybir.AluOpType
+AXIS = mybir.AxisListType
+
+P = 128
+PACK = 4
+WINDOW = 1024
+RUN = 16
+BLOCKS = E // P
+VL_VECTOR_COLUMNS = 176
+
+
+def interleave(copy, grouped, raw, first, last):
+    copy(
+        out=grouped[:, first:last, :].rearrange("p (c i) t -> p c t i", i=4),
+        in_=raw[:, :, first:last].rearrange("p t (c i) -> p c t i", i=4),
+    )
+
+
+def quantize(nc, codes, scales, grouped):
+    nc.vector.quantize_mx(out=codes.bitcast(FP8X4), scales=scales, in_=grouped.rearrange("p w t -> p (w t)"))
+
+
+def product(nc, acc, lhs_codes, lhs_scales, rhs_codes, rhs_scales):
+    nc.tensor.matmul_mx(
+        out=acc,
+        lhsT=lhs_codes.bitcast(FP8X4),
+        lhsT_scale=lhs_scales,
+        rhs=rhs_codes.bitcast(FP8X4),
+        rhs_scale=rhs_scales,
+        start=True,
+        stop=True,
+    )
+
+
+def tile_attend_threelevels_kernel(
+    tc, query, keys_words, keys_scales, pquery, pgsum, vquery, vlsum, size, vals, offs, offs2, offs3, out
+):
+    nc = tc.nc
+    with ExitStack() as ctx:
+        sb = ctx.enter_context(tc.tile_pool(name="sb", bufs=1))
+        ps = ctx.enter_context(tc.psum_pool(name="ps", bufs=1))
+
+        def load_rows(name, rows):
+            raw = sb.tile([P, PACK, rows.shape[1]], F32, name=name)
+            nc.sync.dma_start(out=raw[:], in_=rows.rearrange("(p t) w -> p t w", t=PACK))
+            return raw
+
+        def load_list(name, dram):
+            tile = sb.tile([P, I // 16], U16, name=name)
+            nc.sync.dma_start(tile[:], dram)
+            return tile
+
+        key_bytes = sb.tile([P, T], U8, name="key_bytes", align_bytes=64)
+        nc.gpsimd.memset(key_bytes[:].bitcast(I32), 0)
+        vq_raw = load_rows("vq_raw", vquery)
+        pq_raw = load_rows("pq_raw", pquery)
+        vl_raw = load_rows("vl_raw", vlsum)
+        pg_raw = load_rows("pg_raw", pgsum)
+        volume_list = load_list("volume_list", offs3)
+        page_list = load_list("page_list", offs2)
+        q_raw = load_rows("q_raw", query)
+        key_words = sb.tile([P, T], I32, name="key_words", align_bytes=64)
+        nc.sync.dma_start(out=key_words[:], in_=keys_words[0].rearrange("p n t -> p (n t)").bitcast(I32))
+        for quadrant in range(4):
+            nc.sync.dma_start(
+                out=key_bytes[32 * quadrant : 32 * quadrant + 4, :].bitcast(I32),
+                in_=keys_scales[0, 4 * quadrant : 4 * quadrant + 4, :].bitcast(I32),
+            )
+        token_list = load_list("token_list", offs)
+        size_columns = sb.tile([P, PACK], F32, name="size_columns")
+        nc.sync.dma_start(out=size_columns[:], in_=size.rearrange("o (p j) -> p (o j)", j=PACK))
+        pools = []
+        for j in range(BLOCKS):
+            pool_block = sb.tile([P, T], F32, name="vals%d" % j)
+            nc.sync.dma_start(out=pool_block[:], in_=vals[j * P : (j + 1) * P, :])
+            pools.append(pool_block)
+
+        identity = sb.tile([P, P], F32, name="identity")
+        make_identity(nc, identity[:])
+
+        g_window = sb.tile([P, WINDOW], F32, name="g_window")
+        b_window = sb.tile([P, WINDOW], F32, name="b_window")
+        nc.vector.memset(g_window[:, V:], 0.0)
+        nc.vector.memset(b_window[:, U:], 0.0)
+        warm = sb.tile([P, 1], F32, name="warm")
+        nc.scalar.activation(warm[:], b_window[:, U : U + 1], ACT.Sigmoid)
+
+        lq = sb.tile([P, 2 * Q, PACK], BF16, name="lq", align_bytes=64)
+        lq_codes = sb.tile([P, 2 * Q], U32, name="lq_codes", align_bytes=64)
+        lq_scales = sb.tile([P, 2 * Q], U8, name="lq_scales", align_bytes=64)
+        interleave(nc.vector.tensor_copy, lq[:, :Q, :], vq_raw, 0, Q)
+        interleave(nc.vector.tensor_copy, lq[:, Q:, :], pq_raw, 0, Q)
+        quantize(nc, lq_codes[:], lq_scales[:], lq[:])
+
+        vl = sb.tile([P, V, PACK], BF16, name="vl", align_bytes=64)
+        vl_codes = sb.tile([P, V], U32, name="vl_codes", align_bytes=64)
+        vl_scales = sb.tile([P, V], U8, name="vl_scales", align_bytes=64)
+        interleave(nc.vector.tensor_copy, vl, vl_raw, 0, VL_VECTOR_COLUMNS)
+        interleave(nc.scalar.copy, vl, vl_raw, VL_VECTOR_COLUMNS, V)
+        quantize(nc, vl_codes[:], vl_scales[:], vl[:])
+        g_bank = ps.tile([P, V], F32, name="g_bank")
+        product(nc, g_bank[:], lq_codes[:, :Q], lq_scales[:, :Q], vl_codes[:], vl_scales[:])
+        nc.scalar.copy(out=g_window[:, :V], in_=g_bank[:])
+        g_gate = sb.tile([P, I], F32, name="g_gate")
+        nc.scalar.activation(g_gate[:], g_window[:].indirect(volume_list[:]), ACT.Sigmoid)
+
+        pg = sb.tile([P, U, PACK], BF16, name="pg", align_bytes=64)
+        pg_codes = sb.tile([P, U], U32, name="pg_codes", align_bytes=64)
+        pg_scales = sb.tile([P, U], U8, name="pg_scales", align_bytes=64)
+        interleave(nc.vector.tensor_copy, pg, pg_raw, 0, U)
+        quantize(nc, pg_codes[:], pg_scales[:], pg[:])
+        b_bank = ps.tile([P, U], F32, name="b_bank")
+        product(nc, b_bank[:], lq_codes[:, Q:], lq_scales[:, Q:], pg_codes[:], pg_scales[:])
+        nc.scalar.copy(out=b_window[:, :U], in_=b_bank[:])
+        b_gate = sb.tile([P, I], F32, name="b_gate")
+        nc.scalar.activation(b_gate[:], b_window[:].indirect(page_list[:]), ACT.Sigmoid)
+
+        qg = sb.tile([P, Q, PACK], BF16, name="qg", align_bytes=64)
+        q_codes = sb.tile([P, Q], U32, name="q_codes", align_bytes=64)
+        q_scales = sb.tile([P, Q], U8, name="q_scales", align_bytes=64)
+        interleave(nc.vector.tensor_copy, qg, q_raw, 0, Q)
+        quantize(nc, q_codes[:], q_scales[:], qg[:])
+
+        k_scales = sb.tile([P, I], U8, name="k_scales", align_bytes=64)
+        k_codes = sb.tile([P, I], U32, name="k_codes", align_bytes=64)
+        nc.vector.tensor_copy(k_scales[:], key_bytes[:].indirect(token_list[:]))
+        nc.vector.tensor_copy(k_codes[:], key_words[:].bitcast(U32).indirect(token_list[:]))
+        a_bank = ps.tile([P, I], F32, name="a_bank")
+        product(nc, a_bank[:], q_codes[:], q_scales[:], k_codes[:], k_scales[:])
+
+        v_codes = sb.tile([P, E], U32, name="v_codes", align_bytes=64)
+        v_scales = sb.tile([P, E], U8, name="v_scales", align_bytes=64)
+
+        def turn(name, pairs, bank):
+            words = pairs[:].bitcast(F32)
+            for u in range(2):
+                nc.tensor.transpose(bank[:, u, :], words[:, u * P : (u + 1) * P], identity[:])
+            grouped = sb.tile([P, P, PACK], BF16, name=name, align_bytes=64)
+            nc.scalar.copy(
+                out=grouped[:].rearrange("p x t -> p (x t)").bitcast(F32).rearrange("p (x u) -> p x u", u=2),
+                in_=bank[:].rearrange("p u x -> p x u"),
+            )
+            return grouped
+
+        def gather_values(j):
+            picked = sb.tile([P, I], BF16, name="picked%d" % j, align_bytes=64)
+            nc.vector.tensor_copy(
+                picked[:].rearrange("p (u b r) -> p b u r", u=2, r=RUN), pools[j][:].indirect(token_list[:])
+            )
+            bank = ps.tile([P, 2, P], F32, name="v_bank", bufs=2)
+            return turn("v_grouped%d" % j, picked, bank)
+
+        def quantize_values(j, grouped):
+            quantize(nc, v_codes[:, j * P : (j + 1) * P], v_scales[:, j * P : (j + 1) * P], grouped[:])
+
+        size_bank = ps.tile([P, PACK, P], F32, name="size_bank", tag="spare")
+        for j in range(PACK):
+            nc.tensor.transpose(size_bank[:, j, :], size_columns[:, j : j + 1].to_broadcast([P, P]), identity[:])
+        size_rows = sb.tile([P, I], F32, name="size_rows")
+        nc.scalar.copy(out=size_rows[:].rearrange("p (s j) -> p s j", j=PACK), in_=size_bank[:].rearrange("p j s -> p s j"))
+
+        neg_max = sb.tile([P, 1], F32, name="neg_max")
+        nc.vector.tensor_reduce(neg_max[:], a_bank[:], AXIS.X, ALU.max, negate=True)
+        v0 = gather_values(0)
+        gates = sb.tile([P, I], F32, name="gates")
+        nc.vector.tensor_tensor(gates[:], g_gate[:], b_gate[:], ALU.mult)
+        exps = sb.tile([P, I], F32, name="exps")
+        nc.scalar.activation(exps[:], a_bank[:], ACT.Exp, bias=neg_max[:])
+        quantize_values(0, v0)
+        p = sb.tile([P, I], F32, name="p")
+        row_sum = sb.tile([P, 1], F32, name="row_sum")
+        nc.vector.scalar_tensor_tensor(p[:], exps[:], 1.0, gates[:], ALU.mult, ALU.mult, accum_out=row_sum[:])
+        inverse = sb.tile([P, 1], F32, name="inverse")
+        nc.vector.reciprocal(inverse[:], row_sum[:])
+        w = sb.tile([P, I], BF16, name="w", align_bytes=64)
+        for u in range(2):
+            nc.vector.scalar_tensor_tensor(
+                w[:, u * 256 : (u + 1) * 256].rearrange("p (b r) -> p b r", r=RUN),
+                p[:].rearrange("p (b u r) -> p b u r", u=2, r=RUN)[:, :, u, :],
+                inverse[:],
+                size_rows[:].rearrange("p (b u r) -> p b u r", u=2, r=RUN)[:, :, u, :],
+                ALU.mult,
+                ALU.mult,
+            )
+        w_bank = ps.tile([P, 2, P], F32, name="w_bank", tag="spare")
+        w_grouped = turn("w_grouped", w, w_bank)
+        v1 = gather_values(1)
+        w_codes = sb.tile([P, Q], U32, name="w_codes", align_bytes=64)
+        w_scales = sb.tile([P, Q], U8, name="w_scales", align_bytes=64)
+        quantize(nc, w_codes[:], w_scales[:], w_grouped[:])
+        quantize_values(1, v1)
+
+        result = sb.tile([P, E], F32, name="result")
+
+        def finish(first, last):
+            bank = ps.tile([P, 2 * P], F32, name="o_bank", bufs=2)
+            acc = bank[:, : last - first]
+            product(nc, acc, w_codes[:], w_scales[:], v_codes[:, first:last], v_scales[:, first:last])
+            nc.scalar.copy(out=result[:, first:last], in_=acc)
+            nc.sync.dma_start(out=out[:, first:last], in_=result[:, first:last])
+
+        finish(0, 2 * P)
+        for j in range(2, BLOCKS):
+            quantize_values(j, gather_values(j))
+            finish(j * P, (j + 1) * P)

@@ -22,7 +22,7 @@ PACK = 4
 WINDOW = 1024
 RUN = 16
 BLOCKS = E // P
-VL_VECTOR_COLUMNS = 176
+PG_VECTOR_COLUMNS = 344
 
 
 def interleave(copy, grouped, raw, first, last):
@@ -56,8 +56,8 @@ def tile_attend_threelevels_kernel(
         sb = ctx.enter_context(tc.tile_pool(name="sb", bufs=1))
         ps = ctx.enter_context(tc.psum_pool(name="ps", bufs=1))
 
-        def load_rows(name, rows):
-            raw = sb.tile([P, PACK, rows.shape[1]], F32, name=name)
+        def load_rows(name, rows, tag):
+            raw = sb.tile([P, PACK, rows.shape[1]], F32, name=name, tag=tag, align_bytes=64)
             nc.sync.dma_start(out=raw[:], in_=rows.rearrange("(p t) w -> p t w", t=PACK))
             return raw
 
@@ -66,156 +66,149 @@ def tile_attend_threelevels_kernel(
             nc.sync.dma_start(tile[:], dram)
             return tile
 
-        key_bytes = sb.tile([P, T], U8, name="key_bytes", align_bytes=64)
+        key_bytes = sb.tile([P, T], U8, name="key_bytes", tag="key_bytes", align_bytes=64)
         nc.gpsimd.memset(key_bytes[:].bitcast(I32), 0)
-        vq_raw = load_rows("vq_raw", vquery)
-        pq_raw = load_rows("pq_raw", pquery)
-        vl_raw = load_rows("vl_raw", vlsum)
-        pg_raw = load_rows("pg_raw", pgsum)
-        volume_list = load_list("volume_list", offs3)
+        pq_raw = load_rows("pq_raw", pquery, "stage0")
+        pg_raw = load_rows("pg_raw", pgsum, "stage2")
         page_list = load_list("page_list", offs2)
-        q_raw = load_rows("q_raw", query)
+        vq_raw = load_rows("vq_raw", vquery, "stage1")
+        vl_raw = load_rows("vl_raw", vlsum, "stage3")
+        volume_list = load_list("volume_list", offs3)
+        q_raw = load_rows("q_raw", query, "q_raw")
         key_words = sb.tile([P, T], I32, name="key_words", align_bytes=64)
         nc.sync.dma_start(out=key_words[:], in_=keys_words[0].rearrange("p n t -> p (n t)").bitcast(I32))
-        for quadrant in range(4):
-            nc.sync.dma_start(
-                out=key_bytes[32 * quadrant : 32 * quadrant + 4, :].bitcast(I32),
-                in_=keys_scales[0, 4 * quadrant : 4 * quadrant + 4, :].bitcast(I32),
-            )
         token_list = load_list("token_list", offs)
+        for row in range(4):
+            nc.sync.dma_start(
+                out=key_bytes[row:P:32, :].bitcast(I32),
+                in_=keys_scales[0, row:16:4, :].bitcast(I32),
+            )
         size_columns = sb.tile([P, PACK], F32, name="size_columns")
         nc.sync.dma_start(out=size_columns[:], in_=size.rearrange("o (p j) -> p (o j)", j=PACK))
-        pools = []
-        for j in range(BLOCKS):
-            pool_block = sb.tile([P, T], F32, name="vals%d" % j)
-            nc.sync.dma_start(out=pool_block[:], in_=vals[j * P : (j + 1) * P, :])
-            pools.append(pool_block)
-
         identity = sb.tile([P, P], F32, name="identity")
         make_identity(nc, identity[:])
 
         g_window = sb.tile([P, WINDOW], F32, name="g_window")
         b_window = sb.tile([P, WINDOW], F32, name="b_window")
-        nc.vector.memset(g_window[:, V:], 0.0)
         nc.vector.memset(b_window[:, U:], 0.0)
+        nc.vector.memset(g_window[:, V:], 0.0)
         warm = sb.tile([P, 1], F32, name="warm")
         nc.scalar.activation(warm[:], b_window[:, U : U + 1], ACT.Sigmoid)
 
-        lq = sb.tile([P, 2 * Q, PACK], BF16, name="lq", align_bytes=64)
-        lq_codes = sb.tile([P, 2 * Q], U32, name="lq_codes", align_bytes=64)
-        lq_scales = sb.tile([P, 2 * Q], U8, name="lq_scales", align_bytes=64)
-        interleave(nc.vector.tensor_copy, lq[:, :Q, :], vq_raw, 0, Q)
-        interleave(nc.vector.tensor_copy, lq[:, Q:, :], pq_raw, 0, Q)
-        quantize(nc, lq_codes[:], lq_scales[:], lq[:])
+        def operand(name, width):
+            grouped = sb.tile([P, width, PACK], BF16, name=name, align_bytes=64)
+            codes = sb.tile([P, width], U32, name=name + "_codes", align_bytes=64)
+            scales = sb.tile([P, width], U8, name=name + "_scales", align_bytes=64)
+            return grouped, codes, scales
 
-        vl = sb.tile([P, V, PACK], BF16, name="vl", align_bytes=64)
-        vl_codes = sb.tile([P, V], U32, name="vl_codes", align_bytes=64)
-        vl_scales = sb.tile([P, V], U8, name="vl_scales", align_bytes=64)
-        interleave(nc.vector.tensor_copy, vl, vl_raw, 0, VL_VECTOR_COLUMNS)
-        interleave(nc.scalar.copy, vl, vl_raw, VL_VECTOR_COLUMNS, V)
-        quantize(nc, vl_codes[:], vl_scales[:], vl[:])
-        g_bank = ps.tile([P, V], F32, name="g_bank")
-        product(nc, g_bank[:], lq_codes[:, :Q], lq_scales[:, :Q], vl_codes[:], vl_scales[:])
-        nc.scalar.copy(out=g_window[:, :V], in_=g_bank[:])
-        g_gate = sb.tile([P, I], F32, name="g_gate")
-        nc.scalar.activation(g_gate[:], g_window[:].indirect(volume_list[:]), ACT.Sigmoid)
+        def vector_operand(name, raw):
+            width = raw.shape[2]
+            grouped, codes, scales = operand(name, width)
+            interleave(nc.vector.tensor_copy, grouped, raw, 0, width)
+            quantize(nc, codes[:], scales[:], grouped[:])
+            return codes, scales
 
-        pg = sb.tile([P, U, PACK], BF16, name="pg", align_bytes=64)
-        pg_codes = sb.tile([P, U], U32, name="pg_codes", align_bytes=64)
-        pg_scales = sb.tile([P, U], U8, name="pg_scales", align_bytes=64)
-        interleave(nc.vector.tensor_copy, pg, pg_raw, 0, U)
-        quantize(nc, pg_codes[:], pg_scales[:], pg[:])
-        b_bank = ps.tile([P, U], F32, name="b_bank")
-        product(nc, b_bank[:], lq_codes[:, Q:], lq_scales[:, Q:], pg_codes[:], pg_scales[:])
-        nc.scalar.copy(out=b_window[:, :U], in_=b_bank[:])
+        pq_codes, pq_scales = vector_operand("pq", pq_raw)
+        pg, pg_codes, pg_scales = operand("pg", U)
+        half = U // 2
+        interleave(nc.vector.tensor_copy, pg, pg_raw, 0, half)
+        interleave(nc.vector.tensor_copy, pg, pg_raw, half, PG_VECTOR_COLUMNS)
+        interleave(nc.scalar.copy, pg, pg_raw, PG_VECTOR_COLUMNS, U)
+        for h in range(2):
+            cols = slice(h * half, (h + 1) * half)
+            quantize(nc, pg_codes[:, cols], pg_scales[:, cols], pg[:, cols, :])
+            b_bank = ps.tile([P, half], F32, name="b_bank%d" % h, tag="b_bank%d" % h)
+            product(nc, b_bank[:], pq_codes[:], pq_scales[:], pg_codes[:, cols], pg_scales[:, cols])
+            nc.scalar.copy(out=b_window[:, cols], in_=b_bank[:])
         b_gate = sb.tile([P, I], F32, name="b_gate")
         nc.scalar.activation(b_gate[:], b_window[:].indirect(page_list[:]), ACT.Sigmoid)
 
-        qg = sb.tile([P, Q, PACK], BF16, name="qg", align_bytes=64)
-        q_codes = sb.tile([P, Q], U32, name="q_codes", align_bytes=64)
-        q_scales = sb.tile([P, Q], U8, name="q_scales", align_bytes=64)
-        interleave(nc.vector.tensor_copy, qg, q_raw, 0, Q)
-        quantize(nc, q_codes[:], q_scales[:], qg[:])
+        vq_codes, vq_scales = vector_operand("vq", vq_raw)
+        vl_codes, vl_scales = vector_operand("vl", vl_raw)
+        g_bank = ps.tile([P, V], F32, name="g_bank", tag="g_bank")
+        product(nc, g_bank[:], vq_codes[:], vq_scales[:], vl_codes[:], vl_scales[:])
+        q_codes, q_scales = vector_operand("q", q_raw)
+        nc.vector.tensor_copy(out=g_window[:, :V], in_=g_bank[:])
+        g_gate = sb.tile([P, I], F32, name="g_gate", tag="g_gate", align_bytes=64)
+        nc.scalar.activation(g_gate[:], g_window[:].indirect(volume_list[:]), ACT.Sigmoid)
+
+        pools = []
+        for j in range(BLOCKS):
+            pool_block = sb.tile([P, T], F32, name="vals%d" % j, tag="stage%d" % j, align_bytes=64)
+            nc.sync.dma_start(out=pool_block[:], in_=vals[j * P : (j + 1) * P, :])
+            pools.append(pool_block)
 
         k_scales = sb.tile([P, I], U8, name="k_scales", align_bytes=64)
         k_codes = sb.tile([P, I], U32, name="k_codes", align_bytes=64)
-        nc.vector.tensor_copy(k_scales[:], key_bytes[:].indirect(token_list[:]))
         nc.vector.tensor_copy(k_codes[:], key_words[:].bitcast(U32).indirect(token_list[:]))
-        a_bank = ps.tile([P, I], F32, name="a_bank")
+        nc.vector.tensor_copy(k_scales[:], key_bytes[:].indirect(token_list[:]))
+        a_bank = ps.tile([P, I], F32, name="a_bank", tag="a_bank")
         product(nc, a_bank[:], q_codes[:], q_scales[:], k_codes[:], k_scales[:])
 
-        v_codes = sb.tile([P, E], U32, name="v_codes", align_bytes=64)
-        v_scales = sb.tile([P, E], U8, name="v_scales", align_bytes=64)
+        early = sb.tile([P, BLOCKS * P, PACK], BF16, name="early", align_bytes=64)
+        late = sb.tile([P, P, PACK], BF16, name="late", align_bytes=64)
 
-        def turn(name, pairs, bank):
+        def turn(pairs, bank, grouped):
             words = pairs[:].bitcast(F32)
             for u in range(2):
-                nc.tensor.transpose(bank[:, u, :], words[:, u * P : (u + 1) * P], identity[:])
-            grouped = sb.tile([P, P, PACK], BF16, name=name, align_bytes=64)
+                nc.tensor.transpose(bank[:, u, :], words[:, u : 2 * P : 2], identity[:])
             nc.scalar.copy(
-                out=grouped[:].rearrange("p x t -> p (x t)").bitcast(F32).rearrange("p (x u) -> p x u", u=2),
+                out=grouped.rearrange("p x t -> p (x t)").bitcast(F32).rearrange("p (x u) -> p x u", u=2),
                 in_=bank[:].rearrange("p u x -> p x u"),
             )
-            return grouped
 
-        def gather_values(j):
-            picked = sb.tile([P, I], BF16, name="picked%d" % j, align_bytes=64)
-            nc.vector.tensor_copy(
-                picked[:].rearrange("p (u b r) -> p b u r", u=2, r=RUN), pools[j][:].indirect(token_list[:])
-            )
+        def gather_values(j, grouped, tag):
+            picked = sb.tile([P, I], BF16, name="picked%d" % j, tag=tag, align_bytes=64)
+            nc.vector.tensor_copy(picked[:], pools[j][:].indirect(token_list[:]))
             bank = ps.tile([P, 2, P], F32, name="v_bank", bufs=2)
-            return turn("v_grouped%d" % j, picked, bank)
+            turn(picked, bank, grouped)
 
-        def quantize_values(j, grouped):
-            quantize(nc, v_codes[:, j * P : (j + 1) * P], v_scales[:, j * P : (j + 1) * P], grouped[:])
-
-        size_bank = ps.tile([P, PACK, P], F32, name="size_bank", tag="spare")
+        size_bank = ps.tile([P, PACK, P], F32, name="size_bank")
         for j in range(PACK):
             nc.tensor.transpose(size_bank[:, j, :], size_columns[:, j : j + 1].to_broadcast([P, P]), identity[:])
-        size_rows = sb.tile([P, I], F32, name="size_rows")
-        nc.scalar.copy(out=size_rows[:].rearrange("p (s j) -> p s j", j=PACK), in_=size_bank[:].rearrange("p j s -> p s j"))
 
+        gates = sb.tile([P, I], F32, name="gates", tag="key_bytes", align_bytes=64)
+        nc.vector.tensor_tensor(gates[:], g_gate[:], b_gate[:], ALU.mult)
         neg_max = sb.tile([P, 1], F32, name="neg_max")
         nc.vector.tensor_reduce(neg_max[:], a_bank[:], AXIS.X, ALU.max, negate=True)
-        v0 = gather_values(0)
-        gates = sb.tile([P, I], F32, name="gates")
-        nc.vector.tensor_tensor(gates[:], g_gate[:], b_gate[:], ALU.mult)
         exps = sb.tile([P, I], F32, name="exps")
         nc.scalar.activation(exps[:], a_bank[:], ACT.Exp, bias=neg_max[:])
-        quantize_values(0, v0)
-        p = sb.tile([P, I], F32, name="p")
-        row_sum = sb.tile([P, 1], F32, name="row_sum")
+        gather_values(0, early[:, P : 2 * P, :], "g_gate")
+        p = sb.tile([P, I], F32, name="p", tag="stage0", align_bytes=64)
+        row_sum = sb.tile([P, 1], F32, name="row_sum", tag="row_sum", align_bytes=64)
         nc.vector.scalar_tensor_tensor(p[:], exps[:], 1.0, gates[:], ALU.mult, ALU.mult, accum_out=row_sum[:])
-        inverse = sb.tile([P, 1], F32, name="inverse")
+        inverse = sb.tile([P, 1], F32, name="inverse", tag="inverse", align_bytes=64)
         nc.vector.reciprocal(inverse[:], row_sum[:])
         w = sb.tile([P, I], BF16, name="w", align_bytes=64)
-        for u in range(2):
-            nc.vector.scalar_tensor_tensor(
-                w[:, u * 256 : (u + 1) * 256].rearrange("p (b r) -> p b r", r=RUN),
-                p[:].rearrange("p (b u r) -> p b u r", u=2, r=RUN)[:, :, u, :],
-                inverse[:],
-                size_rows[:].rearrange("p (b u r) -> p b u r", u=2, r=RUN)[:, :, u, :],
-                ALU.mult,
-                ALU.mult,
-            )
-        w_bank = ps.tile([P, 2, P], F32, name="w_bank", tag="spare")
-        w_grouped = turn("w_grouped", w, w_bank)
-        v1 = gather_values(1)
-        w_codes = sb.tile([P, Q], U32, name="w_codes", align_bytes=64)
-        w_scales = sb.tile([P, Q], U8, name="w_scales", align_bytes=64)
-        quantize(nc, w_codes[:], w_scales[:], w_grouped[:])
-        quantize_values(1, v1)
+        nc.vector.scalar_tensor_tensor(
+            w[:].rearrange("p (s j) -> p s j", j=PACK),
+            p[:].rearrange("p (s j) -> p s j", j=PACK),
+            inverse[:],
+            size_bank[:].rearrange("p j s -> p s j"),
+            ALU.mult,
+            ALU.mult,
+        )
+        w_bank = ps.tile([P, 2, P], F32, name="w_bank", tag="b_bank1")
+        turn(w, w_bank, early[:, :P, :])
+        gather_values(1, early[:, 2 * P : 3 * P, :], "row_sum")
+        gather_values(2, early[:, 3 * P :, :], "stage0")
+        gather_values(3, late[:], "inverse")
+
+        early_codes = sb.tile([P, BLOCKS * P], U32, name="early_codes", tag="stage3", align_bytes=64)
+        early_scales = sb.tile([P, BLOCKS * P], U8, name="early_scales", align_bytes=64)
+        late_codes = sb.tile([P, P], U32, name="late_codes", align_bytes=64)
+        late_scales = sb.tile([P, P], U8, name="late_scales", align_bytes=64)
+        quantize(nc, early_codes[:], early_scales[:], early[:])
+        quantize(nc, late_codes[:], late_scales[:], late[:])
 
         result = sb.tile([P, E], F32, name="result")
 
-        def finish(first, last):
-            bank = ps.tile([P, 2 * P], F32, name="o_bank", bufs=2)
-            acc = bank[:, : last - first]
-            product(nc, acc, w_codes[:], w_scales[:], v_codes[:, first:last], v_scales[:, first:last])
-            nc.scalar.copy(out=result[:, first:last], in_=acc)
+        def finish(first, last, codes, scales, tag, copy):
+            bank = ps.tile([P, last - first], F32, name="o_" + tag, tag=tag)
+            product(nc, bank[:], early_codes[:, :P], early_scales[:, :P], codes, scales)
+            copy(out=result[:, first:last], in_=bank[:])
             nc.sync.dma_start(out=out[:, first:last], in_=result[:, first:last])
 
-        finish(0, 2 * P)
-        for j in range(2, BLOCKS):
-            quantize_values(j, gather_values(j))
-            finish(j * P, (j + 1) * P)
+        finish(0, 2 * P, early_codes[:, P : 3 * P], early_scales[:, P : 3 * P], "b_bank0", nc.scalar.copy)
+        finish(2 * P, 3 * P, early_codes[:, 3 * P :], early_scales[:, 3 * P :], "g_bank", nc.scalar.copy)
+        finish(3 * P, 4 * P, late_codes[:], late_scales[:], "a_bank", nc.vector.tensor_copy)

@@ -56,8 +56,8 @@ def tile_attend_threelevels_kernel(
         sb = ctx.enter_context(tc.tile_pool(name="sb", bufs=1))
         ps = ctx.enter_context(tc.psum_pool(name="ps", bufs=1))
 
-        def load_rows(name, rows, tag):
-            raw = sb.tile([P, PACK, rows.shape[1]], F32, name=name, tag=tag, align_bytes=64)
+        def load_rows(name, rows):
+            raw = sb.tile([P, PACK, rows.shape[1]], F32, name=name)
             nc.sync.dma_start(out=raw[:], in_=rows.rearrange("(p t) w -> p t w", t=PACK))
             return raw
 
@@ -68,23 +68,28 @@ def tile_attend_threelevels_kernel(
 
         key_bytes = sb.tile([P, T], U8, name="key_bytes", tag="key_bytes", align_bytes=64)
         nc.gpsimd.memset(key_bytes[:].bitcast(I32), 0)
-        pq_raw = load_rows("pq_raw", pquery, "stage0")
-        pg_raw = load_rows("pg_raw", pgsum, "stage2")
+        pq_raw = load_rows("pq_raw", pquery)
         page_list = load_list("page_list", offs2)
-        vq_raw = load_rows("vq_raw", vquery, "stage1")
-        vl_raw = load_rows("vl_raw", vlsum, "stage3")
+        pg_raw = load_rows("pg_raw", pgsum)
         volume_list = load_list("volume_list", offs3)
-        q_raw = load_rows("q_raw", query, "q_raw")
+        token_list = load_list("token_list", offs)
+        size_columns = sb.tile([P, PACK], F32, name="size_columns")
+        nc.sync.dma_start(out=size_columns[:], in_=size.rearrange("o (p j) -> p (o j)", j=PACK))
+        vq_raw = load_rows("vq_raw", vquery)
+        vl_raw = load_rows("vl_raw", vlsum)
+        q_raw = load_rows("q_raw", query)
         key_words = sb.tile([P, T], I32, name="key_words", align_bytes=64)
         nc.sync.dma_start(out=key_words[:], in_=keys_words[0].rearrange("p n t -> p (n t)").bitcast(I32))
-        token_list = load_list("token_list", offs)
         for row in range(4):
             nc.sync.dma_start(
                 out=key_bytes[row:P:32, :].bitcast(I32),
                 in_=keys_scales[0, row:16:4, :].bitcast(I32),
             )
-        size_columns = sb.tile([P, PACK], F32, name="size_columns")
-        nc.sync.dma_start(out=size_columns[:], in_=size.rearrange("o (p j) -> p (o j)", j=PACK))
+        pools = []
+        for j in range(BLOCKS):
+            pool_block = sb.tile([P, T], F32, name="vals%d" % j, tag="stage%d" % j, align_bytes=64)
+            nc.sync.dma_start(out=pool_block[:], in_=vals[j * P : (j + 1) * P, :])
+            pools.append(pool_block)
         identity = sb.tile([P, P], F32, name="identity")
         make_identity(nc, identity[:])
 
@@ -131,12 +136,6 @@ def tile_attend_threelevels_kernel(
         nc.vector.tensor_copy(out=g_window[:, :V], in_=g_bank[:])
         g_gate = sb.tile([P, I], F32, name="g_gate", tag="g_gate", align_bytes=64)
         nc.scalar.activation(g_gate[:], g_window[:].indirect(volume_list[:]), ACT.Sigmoid)
-
-        pools = []
-        for j in range(BLOCKS):
-            pool_block = sb.tile([P, T], F32, name="vals%d" % j, tag="stage%d" % j, align_bytes=64)
-            nc.sync.dma_start(out=pool_block[:], in_=vals[j * P : (j + 1) * P, :])
-            pools.append(pool_block)
 
         k_scales = sb.tile([P, I], U8, name="k_scales", align_bytes=64)
         k_codes = sb.tile([P, I], U32, name="k_codes", align_bytes=64)

from contextlib import ExitStack

import concourse.mybir as mybir
from concourse.masks import make_identity

D, T, I, Q, E, U, V = 512, 2048, 512, 128, 512, 512, 256
FLOPS = 2 * Q * (D * I + D * U + D * V + I * E)

F32 = mybir.dt.float32
BF16 = mybir.dt.bfloat16
I32 = mybir.dt.int32
U32 = mybir.dt.uint32
U16 = mybir.dt.uint16
U8 = mybir.dt.uint8
FP8X4 = mybir.dt.float8_e4m3fn_x4
ACT = mybir.ActivationFunctionType
ALU = mybir.AluOpType
AXIS = mybir.AxisListType

P = 128
PACK = 4
WINDOW = 1024
RUN = 16
BLOCKS = E // P
PG_VECTOR_COLUMNS = 344


def interleave(copy, grouped, raw, first, last):
    copy(
        out=grouped[:, first:last, :].rearrange("p (c i) t -> p c t i", i=4),
        in_=raw[:, :, first:last].rearrange("p t (c i) -> p c t i", i=4),
    )


def quantize(nc, codes, scales, grouped):
    nc.vector.quantize_mx(out=codes.bitcast(FP8X4), scales=scales, in_=grouped.rearrange("p w t -> p (w t)"))


def product(nc, acc, lhs_codes, lhs_scales, rhs_codes, rhs_scales):
    nc.tensor.matmul_mx(
        out=acc,
        lhsT=lhs_codes.bitcast(FP8X4),
        lhsT_scale=lhs_scales,
        rhs=rhs_codes.bitcast(FP8X4),
        rhs_scale=rhs_scales,
        start=True,
        stop=True,
    )


def tile_attend_threelevels_kernel(
    tc, query, keys_words, keys_scales, pquery, pgsum, vquery, vlsum, size, vals, offs, offs2, offs3, out
):
    nc = tc.nc
    with ExitStack() as ctx:
        sb = ctx.enter_context(tc.tile_pool(name="sb", bufs=1))
        ps = ctx.enter_context(tc.psum_pool(name="ps", bufs=1))

        def load_rows(name, rows):
            raw = sb.tile([P, PACK, rows.shape[1]], F32, name=name)
            nc.sync.dma_start(out=raw[:], in_=rows.rearrange("(p t) w -> p t w", t=PACK))
            return raw

        def load_list(name, dram):
            tile = sb.tile([P, I // 16], U16, name=name)
            nc.sync.dma_start(tile[:], dram)
            return tile

        key_bytes = sb.tile([P, T], U8, name="key_bytes", tag="key_bytes", align_bytes=64)
        nc.gpsimd.memset(key_bytes[:].bitcast(I32), 0)
        pq_raw = load_rows("pq_raw", pquery)
        page_list = load_list("page_list", offs2)
        pg_raw = load_rows("pg_raw", pgsum)
        volume_list = load_list("volume_list", offs3)
        token_list = load_list("token_list", offs)
        size_columns = sb.tile([P, PACK], F32, name="size_columns")
        nc.sync.dma_start(out=size_columns[:], in_=size.rearrange("o (p j) -> p (o j)", j=PACK))
        vq_raw = load_rows("vq_raw", vquery)
        vl_raw = load_rows("vl_raw", vlsum)
        q_raw = load_rows("q_raw", query)
        key_words = sb.tile([P, T], I32, name="key_words", align_bytes=64)
        nc.sync.dma_start(out=key_words[:], in_=keys_words[0].rearrange("p n t -> p (n t)").bitcast(I32))
        for row in range(4):
            nc.sync.dma_start(
                out=key_bytes[row:P:32, :].bitcast(I32),
                in_=keys_scales[0, row:16:4, :].bitcast(I32),
            )
        pools = []
        for j in range(BLOCKS):
            pool_block = sb.tile([P, T], F32, name="vals%d" % j, tag="stage%d" % j, align_bytes=64)
            nc.sync.dma_start(out=pool_block[:], in_=vals[j * P : (j + 1) * P, :])
            pools.append(pool_block)
        identity = sb.tile([P, P], F32, name="identity")
        make_identity(nc, identity[:])

        g_window = sb.tile([P, WINDOW], F32, name="g_window")
        b_window = sb.tile([P, WINDOW], F32, name="b_window")
        nc.vector.memset(b_window[:, U:], 0.0)
        nc.vector.memset(g_window[:, V:], 0.0)
        warm = sb.tile([P, 1], F32, name="warm")
        nc.scalar.activation(warm[:], b_window[:, U : U + 1], ACT.Sigmoid)

        def operand(name, width):
            grouped = sb.tile([P, width, PACK], BF16, name=name, align_bytes=64)
            codes = sb.tile([P, width], U32, name=name + "_codes", align_bytes=64)
            scales = sb.tile([P, width], U8, name=name + "_scales", align_bytes=64)
            return grouped, codes, scales

        def vector_operand(name, raw):
            width = raw.shape[2]
            grouped, codes, scales = operand(name, width)
            interleave(nc.vector.tensor_copy, grouped, raw, 0, width)
            quantize(nc, codes[:], scales[:], grouped[:])
            return codes, scales

        pq_codes, pq_scales = vector_operand("pq", pq_raw)
        pg, pg_codes, pg_scales = operand("pg", U)
        half = U // 2
        interleave(nc.vector.tensor_copy, pg, pg_raw, 0, half)
        interleave(nc.vector.tensor_copy, pg, pg_raw, half, PG_VECTOR_COLUMNS)
        interleave(nc.scalar.copy, pg, pg_raw, PG_VECTOR_COLUMNS, U)
        for h in range(2):
            cols = slice(h * half, (h + 1) * half)
            quantize(nc, pg_codes[:, cols], pg_scales[:, cols], pg[:, cols, :])
            b_bank = ps.tile([P, half], F32, name="b_bank%d" % h, tag="b_bank%d" % h)
            product(nc, b_bank[:], pq_codes[:], pq_scales[:], pg_codes[:, cols], pg_scales[:, cols])
            nc.scalar.copy(out=b_window[:, cols], in_=b_bank[:])
        b_gate = sb.tile([P, I], F32, name="b_gate")
        nc.scalar.activation(b_gate[:], b_window[:].indirect(page_list[:]), ACT.Sigmoid)

        vq_codes, vq_scales = vector_operand("vq", vq_raw)
        vl_codes, vl_scales = vector_operand("vl", vl_raw)
        g_bank = ps.tile([P, V], F32, name="g_bank", tag="g_bank")
        product(nc, g_bank[:], vq_codes[:], vq_scales[:], vl_codes[:], vl_scales[:])
        q_codes, q_scales = vector_operand("q", q_raw)
        nc.vector.tensor_copy(out=g_window[:, :V], in_=g_bank[:])
        g_gate = sb.tile([P, I], F32, name="g_gate", tag="g_gate", align_bytes=64)
        nc.scalar.activation(g_gate[:], g_window[:].indirect(volume_list[:]), ACT.Sigmoid)

        k_scales = sb.tile([P, I], U8, name="k_scales", align_bytes=64)
        k_codes = sb.tile([P, I], U32, name="k_codes", align_bytes=64)
        nc.vector.tensor_copy(k_codes[:], key_words[:].bitcast(U32).indirect(token_list[:]))
        nc.vector.tensor_copy(k_scales[:], key_bytes[:].indirect(token_list[:]))
        a_bank = ps.tile([P, I], F32, name="a_bank", tag="a_bank")
        product(nc, a_bank[:], q_codes[:], q_scales[:], k_codes[:], k_scales[:])

        early = sb.tile([P, BLOCKS * P, PACK], BF16, name="early", align_bytes=64)
        late = sb.tile([P, P, PACK], BF16, name="late", align_bytes=64)

        def turn(pairs, bank, grouped):
            words = pairs[:].bitcast(F32)
            for u in range(2):
                nc.tensor.transpose(bank[:, u, :], words[:, u : 2 * P : 2], identity[:])
            nc.scalar.copy(
                out=grouped.rearrange("p x t -> p (x t)").bitcast(F32).rearrange("p (x u) -> p x u", u=2),
                in_=bank[:].rearrange("p u x -> p x u"),
            )

        def gather_values(j, grouped, tag):
            picked = sb.tile([P, I], BF16, name="picked%d" % j, tag=tag, align_bytes=64)
            nc.vector.tensor_copy(picked[:], pools[j][:].indirect(token_list[:]))
            bank = ps.tile([P, 2, P], F32, name="v_bank", bufs=2)
            turn(picked, bank, grouped)

        size_bank = ps.tile([P, PACK, P], F32, name="size_bank")
        for j in range(PACK):
            nc.tensor.transpose(size_bank[:, j, :], size_columns[:, j : j + 1].to_broadcast([P, P]), identity[:])

        gates = sb.tile([P, I], F32, name="gates", tag="key_bytes", align_bytes=64)
        nc.vector.tensor_tensor(gates[:], g_gate[:], b_gate[:], ALU.mult)
        neg_max = sb.tile([P, 1], F32, name="neg_max")
        nc.vector.tensor_reduce(neg_max[:], a_bank[:], AXIS.X, ALU.max, negate=True)
        exps = sb.tile([P, I], F32, name="exps")
        nc.scalar.activation(exps[:], a_bank[:], ACT.Exp, bias=neg_max[:])
        gather_values(0, early[:, P : 2 * P, :], "g_gate")
        p = sb.tile([P, I], F32, name="p", tag="stage0", align_bytes=64)
        row_sum = sb.tile([P, 1], F32, name="row_sum", tag="row_sum", align_bytes=64)
        nc.vector.scalar_tensor_tensor(p[:], exps[:], 1.0, gates[:], ALU.mult, ALU.mult, accum_out=row_sum[:])
        inverse = sb.tile([P, 1], F32, name="inverse", tag="inverse", align_bytes=64)
        nc.vector.reciprocal(inverse[:], row_sum[:])
        w = sb.tile([P, I], BF16, name="w", align_bytes=64)
        nc.vector.scalar_tensor_tensor(
            w[:].rearrange("p (s j) -> p s j", j=PACK),
            p[:].rearrange("p (s j) -> p s j", j=PACK),
            inverse[:],
            size_bank[:].rearrange("p j s -> p s j"),
            ALU.mult,
            ALU.mult,
        )
        w_bank = ps.tile([P, 2, P], F32, name="w_bank", tag="b_bank1")
        turn(w, w_bank, early[:, :P, :])
        gather_values(1, early[:, 2 * P : 3 * P, :], "row_sum")
        gather_values(2, early[:, 3 * P :, :], "stage0")
        gather_values(3, late[:], "inverse")

        early_codes = sb.tile([P, BLOCKS * P], U32, name="early_codes", tag="stage3", align_bytes=64)
        early_scales = sb.tile([P, BLOCKS * P], U8, name="early_scales", align_bytes=64)
        late_codes = sb.tile([P, P], U32, name="late_codes", align_bytes=64)
        late_scales = sb.tile([P, P], U8, name="late_scales", align_bytes=64)
        quantize(nc, early_codes[:], early_scales[:], early[:])
        quantize(nc, late_codes[:], late_scales[:], late[:])

        result = sb.tile([P, E], F32, name="result")

        def finish(first, last, codes, scales, tag, copy):
            bank = ps.tile([P, last - first], F32, name="o_" + tag, tag=tag)
            product(nc, bank[:], early_codes[:, :P], early_scales[:, :P], codes, scales)
            copy(out=result[:, first:last], in_=bank[:])
            nc.sync.dma_start(out=out[:, first:last], in_=result[:, first:last])

        finish(0, 2 * P, early_codes[:, P : 3 * P], early_scales[:, P : 3 * P], "b_bank0", nc.scalar.copy)
        finish(2 * P, 3 * P, early_codes[:, 3 * P :], early_scales[:, 3 * P :], "g_bank", nc.scalar.copy)
        finish(3 * P, 4 * P, late_codes[:], late_scales[:], "a_bank", nc.vector.tensor_copy)
